import numpy as np, ml_dtypes
CORES = [48,49,50,51,52,53,54,55,72,73,74,75,76,77,78,79]
N = 16
def setup_inputs(rng):
    return {"x": rng.standard_normal((N, 128, 8), dtype=np.float32).astype(ml_dtypes.bfloat16)}
def reference(x):
    s = x.sum(axis=0, dtype=np.float64).astype(x.dtype)
    return {"y": np.broadcast_to(s, (N,) + s.shape)}

@@ -1,0 +1,77 @@
+from concourse.bass import DstId, RemoteDMATransfer
+from concourse.mybir import AluOpType
+
+SCRATCH = {
+    "xs": ("dram", [128, 8], "bfloat16"),
+    "land": ("dram", [8, 128, 8], "bfloat16"),
+    "own": ("dram", [128, 8], "bfloat16"),
+    "oth": ("dram", [128, 8], "bfloat16"),
+}
+SEMAPHORES = ["ld", "arr", "own_in", "oth_in", "st", "acc", "snt"]
+
+HELP_CHIP = {6: 8, 9: 7}
+FEEDS = {8: 9, 7: 6}
+HELP_CORES = (2, 6)
+RED_CORES = (0, 4)
+RED_DSTS = {0: (1, 2, 3, 4), 4: (5, 6, 7, 0)}
+
+
+def eng(lo, n):
+    return ((1 << n) - 1) << lo
+
+
+def rank_program(g, core, T, topo):
+    chip, k = topo.chip(core), core % 8
+    S = T.sem
+
+    def did(c):
+        rid, pid, _se = topo.addr(c)
+        return DstId(rid=rid, pnc=pid)
+
+    if chip in FEEDS:
+        if k not in HELP_CORES:
+            return
+        base = FEEDS[chip] * 8
+        dsts = [base + j for j in (range(0, 4) if k < 4 else range(4, 8))]
+        g.wait_ge(S.arr, 8 * 4)
+        g.remote_dma_fused(
+            [RemoteDMATransfer(dst_ids=[did(d)], dma_engine_mask=eng(2 * i, 2), remote_sem=S.oth_in,
+                               srcs=[T.land[j] for j in range(8)], dsts=[T.oth[:]], alu_op=1)
+             for i, d in enumerate(dsts)],
+            local_sem=S.snt)
+        g.wait_ge(S.snt, 8)
+        return
+
+    if T.rank_of(core) is None:
+        return
+
+    base = chip * 8
+    g.sync.dma_start(T.xs[:], T.x[:]).then_inc(S.ld, 16)
+    g.wait_ge(S.ld, 16)
+    tr = [RemoteDMATransfer(dst_ids=[did(HELP_CHIP[chip] * 8 + h)], dma_engine_mask=eng(4 * i, 4), remote_sem=S.arr,
+                            src=T.xs[:], dst=T.land[k], alu_op=0)
+          for i, h in enumerate(HELP_CORES)]
+    tr += [RemoteDMATransfer(dst_ids=[did(base + r)], dma_engine_mask=eng(8 + 4 * i, 4), remote_sem=S.arr,
+                             src=T.xs[:], dst=T.land[k], alu_op=0)
+           for i, r in enumerate(RED_CORES) if r != k]
+    g.remote_dma_fused(tr, local_sem=S.snt)
+    sent = 4 * len(tr)
+
+    if k in RED_CORES:
+        g.wait_ge(S.arr, 7 * 4)
+        srcs = [T.xs[:] if j == k else T.land[j] for j in range(8)]
+        g.remote_dma_fused(
+            [RemoteDMATransfer(dst_ids=[did(base + d)], dma_engine_mask=eng(4 * i, 4), remote_sem=S.own_in,
+                               srcs=srcs, dsts=[T.own[:]], alu_op=1)
+             for i, d in enumerate(RED_DSTS[k])],
+            local_sem=S.snt)
+        sent += 16
+
+    g.sync.wait_ge(S.own_in, 4)
+    g.sync.dma_start(T.y[:], T.own[:]).then_inc(S.st, 16)
+
+    g.wait_ge(S.snt, sent)
+    g.wait_ge(S.st, 16)
+    g.wait_ge(S.oth_in, 2)
+    g.dma_start(T.y[:], T.oth[:], accum_op=AluOpType.add).then_inc(S.acc, 16)
+    g.wait_ge(S.acc, 16)

@@ -14,6 +14,9 @@ FEEDS = {8: 9, 7: 6}
 HELP_CORES = (2, 6)
 RED_CORES = (0, 4)
 RED_DSTS = {0: (1, 2, 3, 4), 4: (5, 6, 7, 0)}
+OTH_ONE = False
+OWN_ONE = False
+X_ONE = True
 
 
 def eng(lo, n):
@@ -28,17 +31,27 @@ def rank_program(g, core, T, topo):
         rid, pid, _se = topo.addr(c)
         return DstId(rid=rid, pnc=pid)
 
+    def spread(srcs, dsts, buf, sem, lo, engines, one):
+        op = 1 if len(srcs) > 1 else 0
+        if one:
+            return [RemoteDMATransfer(dst_ids=[did(d) for d in dsts], dma_engine_mask=eng(lo, engines),
+                                      remote_sem=sem, srcs=srcs, dsts=[buf for d in dsts], alu_op=op)]
+        n = engines // 4 if op else engines // 2
+        return [RemoteDMATransfer(dst_ids=[did(d)], dma_engine_mask=eng(lo + n * i, n), remote_sem=sem,
+                                  srcs=srcs, dsts=[buf], alu_op=op) for i, d in enumerate(dsts)]
+
+    oth_n = 8 if OTH_ONE else 2
+    own_n = 16 if OWN_ONE else 4
+    x_n = 8 if X_ONE else 4
+
     if chip in FEEDS:
         if k not in HELP_CORES:
             return
         base = FEEDS[chip] * 8
         dsts = [base + j for j in (range(0, 4) if k < 4 else range(4, 8))]
-        g.wait_ge(S.arr, 8 * 4)
-        g.remote_dma_fused(
-            [RemoteDMATransfer(dst_ids=[did(d)], dma_engine_mask=eng(2 * i, 2), remote_sem=S.oth_in,
-                               srcs=[T.land[j] for j in range(8)], dsts=[T.oth[:]], alu_op=1)
-             for i, d in enumerate(dsts)],
-            local_sem=S.snt)
+        g.wait_ge(S.arr, 8 * x_n)
+        g.remote_dma_fused(spread([T.land[j] for j in range(8)], dsts, T.oth[:], S.oth_in, 0, 8, OTH_ONE),
+                           local_sem=S.snt)
         g.wait_ge(S.snt, 8)
         return
 
@@ -48,30 +61,23 @@ def rank_program(g, core, T, topo):
     base = chip * 8
     g.sync.dma_start(T.xs[:], T.x[:]).then_inc(S.ld, 16)
     g.wait_ge(S.ld, 16)
-    tr = [RemoteDMATransfer(dst_ids=[did(HELP_CHIP[chip] * 8 + h)], dma_engine_mask=eng(4 * i, 4), remote_sem=S.arr,
-                            src=T.xs[:], dst=T.land[k], alu_op=0)
-          for i, h in enumerate(HELP_CORES)]
-    tr += [RemoteDMATransfer(dst_ids=[did(base + r)], dma_engine_mask=eng(8 + 4 * i, 4), remote_sem=S.arr,
-                             src=T.xs[:], dst=T.land[k], alu_op=0)
-           for i, r in enumerate(RED_CORES) if r != k]
-    g.remote_dma_fused(tr, local_sem=S.snt)
-    sent = 4 * len(tr)
+    cross = spread([T.xs[:]], [HELP_CHIP[chip] * 8 + h for h in HELP_CORES], T.land[k], S.arr, 0, 8, X_ONE)
+    onchip = spread([T.xs[:]], [base + r for r in RED_CORES if r != k], T.land[k], S.arr, 8, 8, X_ONE)
+    g.remote_dma_fused(cross + onchip, local_sem=S.snt)
+    sent = x_n * (len(cross) + len(onchip))
 
     if k in RED_CORES:
-        g.wait_ge(S.arr, 7 * 4)
-        srcs = [T.xs[:] if j == k else T.land[j] for j in range(8)]
-        g.remote_dma_fused(
-            [RemoteDMATransfer(dst_ids=[did(base + d)], dma_engine_mask=eng(4 * i, 4), remote_sem=S.own_in,
-                               srcs=srcs, dsts=[T.own[:]], alu_op=1)
-             for i, d in enumerate(RED_DSTS[k])],
-            local_sem=S.snt)
+        g.wait_ge(S.arr, 7 * x_n)
+        g.remote_dma_fused(spread([T.xs[:] if j == k else T.land[j] for j in range(8)],
+                                  [base + d for d in RED_DSTS[k]], T.own[:], S.own_in, 0, 16, OWN_ONE),
+                           local_sem=S.snt)
         sent += 16
 
-    g.sync.wait_ge(S.own_in, 4)
+    g.sync.wait_ge(S.own_in, own_n)
     g.sync.dma_start(T.y[:], T.own[:]).then_inc(S.st, 16)
 
     g.wait_ge(S.snt, sent)
     g.wait_ge(S.st, 16)
-    g.wait_ge(S.oth_in, 2)
+    g.wait_ge(S.oth_in, oth_n)
     g.dma_start(T.y[:], T.oth[:], accum_op=AluOpType.add).then_inc(S.acc, 16)
     g.wait_ge(S.acc, 16)

@@ -14,9 +14,6 @@ FEEDS = {8: 9, 7: 6}
 HELP_CORES = (2, 6)
 RED_CORES = (0, 4)
 RED_DSTS = {0: (1, 2, 3, 4), 4: (5, 6, 7, 0)}
-OTH_ONE = False
-OWN_ONE = False
-X_ONE = True
 
 
 def eng(lo, n):
@@ -31,27 +28,17 @@ def rank_program(g, core, T, topo):
         rid, pid, _se = topo.addr(c)
         return DstId(rid=rid, pnc=pid)
 
-    def spread(srcs, dsts, buf, sem, lo, engines, one):
-        op = 1 if len(srcs) > 1 else 0
-        if one:
-            return [RemoteDMATransfer(dst_ids=[did(d) for d in dsts], dma_engine_mask=eng(lo, engines),
-                                      remote_sem=sem, srcs=srcs, dsts=[buf for d in dsts], alu_op=op)]
-        n = engines // 4 if op else engines // 2
-        return [RemoteDMATransfer(dst_ids=[did(d)], dma_engine_mask=eng(lo + n * i, n), remote_sem=sem,
-                                  srcs=srcs, dsts=[buf], alu_op=op) for i, d in enumerate(dsts)]
-
-    oth_n = 8 if OTH_ONE else 2
-    own_n = 16 if OWN_ONE else 4
-    x_n = 8 if X_ONE else 4
+    def spread(srcs, dsts, buf, sem, lo, engines):
+        return RemoteDMATransfer(dst_ids=[did(d) for d in dsts], dma_engine_mask=eng(lo, engines), remote_sem=sem,
+                                 srcs=srcs, dsts=[buf for d in dsts], alu_op=1 if len(srcs) > 1 else 0)
 
     if chip in FEEDS:
         if k not in HELP_CORES:
             return
         base = FEEDS[chip] * 8
         dsts = [base + j for j in (range(0, 4) if k < 4 else range(4, 8))]
-        g.wait_ge(S.arr, 8 * x_n)
-        g.remote_dma_fused(spread([T.land[j] for j in range(8)], dsts, T.oth[:], S.oth_in, 0, 8, OTH_ONE),
-                           local_sem=S.snt)
+        g.wait_ge(S.arr, 8 * 8)
+        g.remote_dma_fused([spread([T.land[j] for j in range(8)], dsts, T.oth[:], S.oth_in, 0, 8)], local_sem=S.snt)
         g.wait_ge(S.snt, 8)
         return
 
@@ -61,23 +48,23 @@ def rank_program(g, core, T, topo):
     base = chip * 8
     g.sync.dma_start(T.xs[:], T.x[:]).then_inc(S.ld, 16)
     g.wait_ge(S.ld, 16)
-    cross = spread([T.xs[:]], [HELP_CHIP[chip] * 8 + h for h in HELP_CORES], T.land[k], S.arr, 0, 8, X_ONE)
-    onchip = spread([T.xs[:]], [base + r for r in RED_CORES if r != k], T.land[k], S.arr, 8, 8, X_ONE)
-    g.remote_dma_fused(cross + onchip, local_sem=S.snt)
-    sent = x_n * (len(cross) + len(onchip))
+    g.remote_dma_fused(
+        [spread([T.xs[:]], [HELP_CHIP[chip] * 8 + h for h in HELP_CORES], T.land[k], S.arr, 0, 8),
+         spread([T.xs[:]], [base + r for r in RED_CORES if r != k], T.land[k], S.arr, 8, 8)],
+        local_sem=S.snt)
+    sent = 16
 
     if k in RED_CORES:
-        g.wait_ge(S.arr, 7 * x_n)
-        g.remote_dma_fused(spread([T.xs[:] if j == k else T.land[j] for j in range(8)],
-                                  [base + d for d in RED_DSTS[k]], T.own[:], S.own_in, 0, 16, OWN_ONE),
-                           local_sem=S.snt)
+        g.wait_ge(S.arr, 7 * 8)
+        g.remote_dma_fused([spread([T.xs[:] if j == k else T.land[j] for j in range(8)],
+                                   [base + d for d in RED_DSTS[k]], T.own[:], S.own_in, 0, 16)], local_sem=S.snt)
         sent += 16
 
-    g.sync.wait_ge(S.own_in, own_n)
+    g.sync.wait_ge(S.own_in, 16)
     g.sync.dma_start(T.y[:], T.own[:]).then_inc(S.st, 16)
 
     g.wait_ge(S.snt, sent)
     g.wait_ge(S.st, 16)
-    g.wait_ge(S.oth_in, oth_n)
+    g.wait_ge(S.oth_in, 8)
     g.dma_start(T.y[:], T.oth[:], accum_op=AluOpType.add).then_inc(S.acc, 16)
     g.wait_ge(S.acc, 16)

from concourse.bass import DstId, RemoteDMATransfer
from concourse.mybir import AluOpType

SCRATCH = {
    "xs": ("dram", [128, 8], "bfloat16"),
    "land": ("dram", [8, 128, 8], "bfloat16"),
    "own": ("dram", [128, 8], "bfloat16"),
    "oth": ("dram", [128, 8], "bfloat16"),
}
SEMAPHORES = ["ld", "arr", "own_in", "oth_in", "st", "acc", "snt"]

HELP_CHIP = {6: 8, 9: 7}
FEEDS = {8: 9, 7: 6}
HELP_CORES = (2, 6)
RED_CORES = (0, 4)
RED_DSTS = {0: (1, 2, 3, 4), 4: (5, 6, 7, 0)}


def eng(lo, n):
    return ((1 << n) - 1) << lo


def rank_program(g, core, T, topo):
    chip, k = topo.chip(core), core % 8
    S = T.sem

    def did(c):
        rid, pid, _se = topo.addr(c)
        return DstId(rid=rid, pnc=pid)

    def spread(srcs, dsts, buf, sem, lo, engines):
        return RemoteDMATransfer(dst_ids=[did(d) for d in dsts], dma_engine_mask=eng(lo, engines), remote_sem=sem,
                                 srcs=srcs, dsts=[buf for d in dsts], alu_op=1 if len(srcs) > 1 else 0)

    if chip in FEEDS:
        if k not in HELP_CORES:
            return
        base = FEEDS[chip] * 8
        dsts = [base + j for j in (range(0, 4) if k < 4 else range(4, 8))]
        g.wait_ge(S.arr, 8 * 8)
        g.remote_dma_fused([spread([T.land[j] for j in range(8)], dsts, T.oth[:], S.oth_in, 0, 8)], local_sem=S.snt)
        g.wait_ge(S.snt, 8)
        return

    if T.rank_of(core) is None:
        return

    base = chip * 8
    g.sync.dma_start(T.xs[:], T.x[:]).then_inc(S.ld, 16)
    g.wait_ge(S.ld, 16)
    g.remote_dma_fused(
        [spread([T.xs[:]], [HELP_CHIP[chip] * 8 + h for h in HELP_CORES], T.land[k], S.arr, 0, 8),
         spread([T.xs[:]], [base + r for r in RED_CORES if r != k], T.land[k], S.arr, 8, 8)],
        local_sem=S.snt)
    sent = 16

    if k in RED_CORES:
        g.wait_ge(S.arr, 7 * 8)
        g.remote_dma_fused([spread([T.xs[:] if j == k else T.land[j] for j in range(8)],
                                   [base + d for d in RED_DSTS[k]], T.own[:], S.own_in, 0, 16)], local_sem=S.snt)
        sent += 16

    g.sync.wait_ge(S.own_in, 16)
    g.sync.dma_start(T.y[:], T.own[:]).then_inc(S.st, 16)

    g.wait_ge(S.snt, sent)
    g.wait_ge(S.st, 16)
    g.wait_ge(S.oth_in, 8)
    g.dma_start(T.y[:], T.oth[:], accum_op=AluOpType.add).then_inc(S.acc, 16)
    g.wait_ge(S.acc, 16)
